import numpy as np, ml_dtypes
CORES = [12,28,60,100,156,228]
N = 6
import mx_ref
NC, G = 128, 4
C = np.float32(0.029)
BF = ml_dtypes.bfloat16
def cut(t, i, w=512):
    return t[:, w * i:w * i + w]
def tile(rs):
    return np.stack(rs, axis=2).reshape(128, -1).astype(BF)
def layer(w, X):
    out = []
    for i in range(G):
        for t in range(len(X)):
            p = mx_ref.matmul(mx_ref.quantize(cut(w, len(X) * i + t)), X[t])
            z = p if t == 0 else z + p
        out.append(z)
    return out
def masked(A, E):
    return [(e * (a > 0)) * C for a, e in zip(A, E)]
def setup_inputs(rng):
    def f(*shape):
        return mx_ref.flush((rng.standard_normal(shape, dtype=np.float32) * np.exp2(rng.integers(-2, 3, shape[:-1] + (1,)))).astype(BF))
    return {"x": f(N, 128, 512), "e": f(N, 128, 512), "a": f(N, 128, G * 512), "w": f(N, 128, 512), "v": f(N, 128, 4 * NC)}
def setup_inputs_blocks(rng):
    d = setup_inputs(rng)
    for k in ("x", "e", "a", "w", "v"): d[k] = mx_ref.spread(d[k], rng, 2)
    return d
def setup_inputs_wide(rng):
    d = setup_inputs(rng)
    for k in ("x", "e", "a", "w", "v"): d[k] = mx_ref.flush((d[k].astype(np.float32) * np.exp2(rng.integers(-6, 7, (N, 1, 1))).astype(np.float32)).astype(BF))
    return d
def setup_inputs_zeros(rng):
    d = setup_inputs(rng); v = d["x"].reshape(N, 128, -1, 4).copy()
    v[np.broadcast_to((rng.random((N, 1, v.shape[2], 1)) < 0.33), v.shape)] = 0
    d["x"] = v.reshape(d["x"].shape)
    return d
def reference(x, e, a, w, v):
    T = [mx_ref.quantize(tile(masked(layer(a[j], [mx_ref.quantize(x[j])]), layer(a[j], [mx_ref.quantize(e[j])])))) for j in range(N)]
    y = np.zeros((N, 128, N * 128), np.float32); z = np.zeros((N, 128, NC), np.float32)
    for r in range(N):
        qw = mx_ref.quantize(w[r]); qv = mx_ref.quantize(v[r])
        for j in range(N):
            y[r][:, 128 * j:128 * j + 128] = mx_ref.matmul(qw, T[j])
            p = mx_ref.matmul(T[j], qv)
            z[r] = p if j == 0 else z[r] + p
    return {"y": y, "z": z}

from concourse.bass import DstId, RemoteDMATransfer
from concourse.mybir import dt, AluOpType, ActivationFunctionType

SIM_CORES = 256
N = 6
NC = 128
C = 0.029

SCRATCH = {
    "xe": ("sbuf", [128, 1024], "bfloat16"),
    "ab": ("sbuf", [128, 2048], "bfloat16"),
    "wv": ("sbuf", [128, 1024], "bfloat16"),
    "tb": ("sbuf", [128, 512], "bfloat16"),
    "mk": ("sbuf", [128, 512], "float32"),
    "ysb": ("sbuf", [128, N * NC], "float32"),
    "zsb": ("sbuf", [128, NC], "float32"),
    "qxe": ("sbuf", [128, 256], "float8_e4m3fn_x4"),
    "sxe": ("sbuf", [128, 256], "uint8"),
    "qa": ("sbuf", [128, 512], "float8_e4m3fn_x4"),
    "sa": ("sbuf", [128, 512], "uint8"),
    "qwv": ("sbuf", [128, 256], "float8_e4m3fn_x4"),
    "swv": ("sbuf", [128, 256], "uint8"),
    "qt": ("sbuf", [128, N * NC], "float8_e4m3fn_x4"),
    "st": ("sbuf", [128, N * NC], "uint8"),
    "rc": ("sbuf", [128, NC], "float8_e4m3fn_x4"),
    "rs": ("sbuf", [128, NC], "uint8"),
}
for _i in range(8):
    SCRATCH["p%d" % _i] = ("psum", [128, 512], "float32")

SEMAPHORES = (["lx", "le", "lw", "lv", "qx", "tq", "qw", "qv", "sent", "relay", "u3", "d3", "zm", "cz", "sz"]
              + ["la%d" % i for i in range(4)] + ["qa%d" % i for i in range(4)] + ["mm%d" % i for i in range(3)]
              + ["k%d" % i for i in range(4)] + ["r%d" % i for i in range(4)]
              + ["arr%d" % i for i in range(N)] + ["ym%d" % i for i in range(N)] + ["cy%d" % i for i in range(N)]
              + ["sy%d" % i for i in range(N)])


def bits(mask):
    return [i for i in range(mask.bit_length()) if mask >> i & 1]


def mask_of(engines):
    return sum(1 << i for i in engines)


def plan(s, T, topo):
    src = T.cores[s]
    order = [(s + i) % N for i in range(1, N)]
    direct = [j for j in order if topo.may_write(src, T.cores[j])]
    cross = sorted(j for j in order if j not in direct)
    place = sorted(direct + [s]).index(s)
    half = (len(cross) + 1) // 2
    parts = [cross[:half], cross[half:]]
    if place % 2:
        parts.reverse()
    own_chip = [c for c in range(SIM_CORES) if topo.host(c) == topo.host(src) and topo.chip(c) == topo.chip(src) and c != src]
    ports = [c for c in own_chip if all(topo.may_write(c, T.cores[j]) for j in cross)]
    near = [c for c in ports if topo.die(c) == topo.die(src)]
    far = [c for c in ports if topo.die(c) != topo.die(src)]
    return direct, cross, [(near[0], near[1], parts[0]), (far[0], far[1], parts[1])]


def ids(topo, src, dsts):
    out = []
    for d in dsts:
        rid, pid = topo.addr(d, src)
        out.append(DstId(rid=rid, pnc=pid))
    return out


def blk(j):
    return slice(NC * j, NC * j + NC)


def rank_program(g, core, T, topo):
    rank = T.rank_of(core)
    if rank is None:
        relay_program(g, core, T, topo)
        return
    S = T.sem
    direct, cross, dies = plan(rank, T, topo)

    g.sync.dma_start(T.xe[:, 0:512], T.x[:, :]).then_inc(S.lx, 16)
    g.scalar.dma_start(T.xe[:, 512:1024], T.e[:, :]).then_inc(S.le, 16)
    for i in range(4):
        q = g.sync if i % 2 == 0 else g.scalar
        q.dma_start(T.ab[:, 512 * i:512 * i + 512], T.a[:, 512 * i:512 * i + 512]).then_inc(S["la%d" % i], 16)
    g.sync.dma_start(T.wv[:, 0:512], T.w[:, :]).then_inc(S.lw, 16)
    g.scalar.dma_start(T.wv[:, 512:1024], T.v[:, :]).then_inc(S.lv, 16)

    v = g.vector
    U = [T.p0, T.p1, T.p2, T.p3]
    D = [T.p0, T.p1, T.p2, T.p4]
    dof = [128, 128, 128, 0]

    def quant_a(i):
        v.wait_ge(S["la%d" % i], 16)
        v.quantize_mx(T.qa[:, blk(i)], T.sa[:, blk(i)], T.ab[:, 512 * i:512 * i + 512]).then_inc(S["qa%d" % i], 1)

    def mask(b):
        v.wait_ge(S["mm%d" % b] if b < 3 else S.u3, 1)
        v.tensor_scalar(T.mk[:, blk(b)], U[b][:, 0:128], 0.0, C, AluOpType.is_gt, AluOpType.mult).then_inc(S["k%d" % b], 1)

    def make(b):
        if b == 3:
            v.wait_ge(S.d3, 1)
        v.wait_ge(S["k%d" % b], 1)
        v.tensor_tensor(T.tb[:, b:512:4], T.mk[:, blk(b)], D[b][:, dof[b]:dof[b] + 128], AluOpType.mult).then_inc(S["r%d" % b], 1)

    v.wait_ge(S.lx, 16)
    v.wait_ge(S.le, 16)
    v.quantize_mx(T.qxe[:, :], T.sxe[:, :], T.xe[:, :]).then_inc(S.qx, 1)
    quant_a(0)
    quant_a(1)
    mask(0)
    make(0)
    quant_a(2)
    mask(1)
    make(1)
    quant_a(3)
    mask(2)
    mask(3)
    make(2)
    make(3)
    for b in range(4):
        v.wait_ge(S["r%d" % b], 1)
    v.quantize_mx(T.qt[:, blk(rank)], T.st[:, blk(rank)], T.tb[:, :]).then_inc(S.tq, 1)
    v.wait_ge(S.lw, 16)
    v.quantize_mx(T.qwv[:, 0:128], T.swv[:, 0:128], T.wv[:, 0:512]).then_inc(S.qw, 1)
    v.wait_ge(S.lv, 16)
    v.quantize_mx(T.qwv[:, 128:256], T.swv[:, 128:256], T.wv[:, 512:1024]).then_inc(S.qv, 1)

    t = g.tensor
    t.wait_ge(S.qx, 1)
    for i in range(3):
        t.wait_ge(S["qa%d" % i], 1)
        t.matmul_mx(U[i][:, 0:256], T.qa[:, blk(i)], T.sa[:, blk(i)], T.qxe[:, 0:256], T.sxe[:, 0:256], True, True).then_inc(S["mm%d" % i], 1)
    t.wait_ge(S.qa3, 1)
    t.matmul_mx(T.p3[:, 0:128], T.qa[:, blk(3)], T.sa[:, blk(3)], T.qxe[:, 0:128], T.sxe[:, 0:128], True, True).then_inc(S.u3, 1)
    t.matmul_mx(T.p4[:, 0:128], T.qa[:, blk(3)], T.sa[:, blk(3)], T.qxe[:, 128:256], T.sxe[:, 128:256], True, True).then_inc(S.d3, 1)

    codes = T.qt[:, blk(rank)].bitcast(dt.uint8)
    plane = T.st[:, blk(rank)]
    off = bits(topo.mask(core, T.cores[direct[0]]))
    on = [i for i in bits(topo.mask(core, dies[0][0])) if i not in off]
    arr = S["arr%d" % rank]
    dcores = [T.cores[j] for j in direct]

    def straight(src, land, engines):
        return RemoteDMATransfer(dst_ids=ids(topo, core, dcores), dma_engine_mask=mask_of(engines), remote_sem=arr,
                                 srcs=[src], dsts=[land] * len(dcores))

    def to_relays(src, land, relays, engines):
        return RemoteDMATransfer(dst_ids=ids(topo, core, relays), dma_engine_mask=mask_of(engines), remote_sem=S.relay,
                                 srcs=[src], dsts=[land] * len(relays))

    rc = T.rc[:, :].bitcast(dt.uint8)
    rs = T.rs[:, :]
    code_relays = [d[0] for d in dies]
    plane_relays = [d[1] for d in dies]
    g.wait_ge(S.tq, 1)
    if len(direct) >= len(cross):
        g.remote_dma_fused([to_relays(codes, rc, code_relays, on), straight(codes, codes, off)], local_sem=S.sent)
        g.remote_dma_fused([to_relays(plane, rs, plane_relays, on), straight(plane, plane, off)], local_sem=S.sent)
        sent = 2 * (len(on) + len(off))
    else:
        g.remote_dma_fused([to_relays(codes, rc, code_relays[:1], on), to_relays(codes, rc, code_relays[1:], off)], local_sem=S.sent)
        g.remote_dma_fused([to_relays(plane, rs, plane_relays[:1], on), to_relays(plane, rs, plane_relays[1:], off)], local_sem=S.sent)
        g.remote_dma_fused([straight(codes, codes, off)], local_sem=S.sent)
        g.remote_dma_fused([straight(plane, plane, off)], local_sem=S.sent)
        sent = 2 * (len(on) + len(off)) + 2 * len(off)
    g.wait_ge(S.sent, sent)

    order = [rank] + direct[::-1] + cross
    banks = [T.p6, T.p7, T.p0, T.p1, T.p2, T.p3]
    for k, j in enumerate(order):
        if k == 0:
            t.wait_ge(S.tq, 1)
            t.wait_ge(S.qw, 1)
        else:
            t.wait_ge(S["arr%d" % j], 2 * len(off))
        t.matmul_mx(banks[k][:, 0:128], T.qwv[:, 0:128], T.swv[:, 0:128], T.qt[:, blk(j)], T.st[:, blk(j)], True, True).then_inc(S["ym%d" % k], 1)
        if k == 0:
            t.wait_ge(S.qv, 1)
        mm = t.matmul_mx(T.p5[:, 0:128], T.qt[:, blk(j)], T.st[:, blk(j)], T.qwv[:, 128:256], T.swv[:, 128:256], k == 0, k == N - 1)
        if k == N - 1:
            mm.then_inc(S.zm, 1)

    for k, j in enumerate(order):
        if k % 2 == 0:
            v.wait_ge(S["ym%d" % k], 1)
            v.tensor_copy(T.ysb[:, blk(j)], banks[k][:, 0:128]).then_inc(S["cy%d" % k], 1)
        else:
            g.scalar.wait_ge(S["ym%d" % k], 1)
            g.scalar.activation(T.ysb[:, blk(j)], banks[k][:, 0:128], ActivationFunctionType.Copy).then_inc(S["cy%d" % k], 1)
    v.wait_ge(S.zm, 1)
    v.tensor_copy(T.zsb[:, :], T.p5[:, 0:128]).then_inc(S.cz, 1)

    def runs(blocks):
        out = []
        for j in sorted(blocks):
            if out and out[-1][-1] == j - 1:
                out[-1].append(j)
            else:
                out.append([j])
        return out

    early = runs([rank] + direct)
    late = []
    for i in range(0, len(cross) - 1, 2):
        late += runs(cross[i:min(i + 2, len(cross) - 1)])
    groups = early + late
    for n, grp in enumerate(groups):
        for j in grp:
            g.sync.wait_ge(S["cy%d" % order.index(j)], 1)
        a, b = NC * grp[0], NC * grp[-1] + NC
        g.sync.dma_start(T.y[:, a:b], T.ysb[:, a:b]).then_inc(S["sy%d" % n], 16)
    last = order[-1]
    g.scalar.wait_ge(S["cy%d" % (N - 1)], 1)
    g.scalar.dma_start(T.y[:, blk(last)], T.ysb[:, blk(last)]).then_inc(S["sy%d" % len(groups)], 16)
    g.sync.wait_ge(S.cz, 1)
    g.sync.dma_start(T.z[:, :], T.zsb[:, :]).then_inc(S.sz, 16)
    for n in range(len(groups)):
        g.sync.wait_ge(S["sy%d" % n], 16)
    g.sync.wait_ge(S.sz, 16)
    g.scalar.wait_ge(S["sy%d" % len(groups)], 16)


def relay_program(g, core, T, topo):
    for s in range(N):
        src = T.cores[s]
        if topo.host(src) != topo.host(core) or topo.chip(src) != topo.chip(core):
            continue
        for code_core, plane_core, part in plan(s, T, topo)[2]:
            if core not in (code_core, plane_core):
                continue
            if core == code_core:
                out, land = T.rc[:, :].bitcast(dt.uint8), T.qt[:, blk(s)].bitcast(dt.uint8)
            else:
                out, land = T.rs[:, :], T.st[:, blk(s)]
            dsts = [T.cores[j] for j in part]
            engines = bits(topo.mask(core, dsts[0]))
            g.wait_ge(T.sem.relay, len(bits(topo.mask(src, core))) // 2)
            g.remote_dma_fused([RemoteDMATransfer(dst_ids=ids(topo, core, dsts), dma_engine_mask=mask_of(engines),
                                                  remote_sem=T.sem["arr%d" % s], srcs=[out], dsts=[land] * len(dsts))],
                               local_sem=T.sem.sent)
            g.wait_ge(T.sem.sent, len(engines))
